import numpy as np
import ml_dtypes


def mxq(x, axis, fmt="e4m3"):
    dtype, down = {"e4m3": (ml_dtypes.float8_e4m3fn, 7), "e5m2": (ml_dtypes.float8_e5m2, 14)}[fmt]
    v = np.moveaxis(np.asarray(x, np.float32).astype(ml_dtypes.bfloat16).astype(np.float64), axis, -1)
    blocks = v.reshape(v.shape[:-1] + (-1, 32))
    amax = np.abs(blocks).max(-1, keepdims=True)
    byte = np.maximum(np.where(amax > 0, np.frexp(amax)[1] - 1 + 127, 0) - down, 1)
    scale = np.exp2(byte - 127.0)
    codes = (blocks / scale).astype(np.float32).astype(dtype).astype(np.float64)
    return np.moveaxis((codes * scale).reshape(v.shape), -1, axis)


WIDE = False


def mx_kscale(k):
    if not WIDE:
        return np.ones(k)
    levels = np.array([10, -10, 5, -5, 0])
    if k % 512:
        return np.exp2(np.random.permutation(np.resize(levels, k // 32))).repeat(32)
    a = np.empty((k // 512, 16))
    for p in range(k // 512):
        a[p, :8] = np.random.permutation(np.resize(levels, 8))
        for g in range(8):
            far = levels[np.abs(levels - a[p, g]) >= 10]
            a[p, g + 8] = far[np.random.randint(len(far))]
    return np.exp2(a.ravel()).repeat(32)


BF16 = ml_dtypes.bfloat16


def bf(x):
    return np.asarray(x, np.float32).astype(BF16)


def f64(x):
    return np.asarray(x).astype(np.float64)


E2M1 = np.array([0.0, 0.5, 1.0, 1.5, 2.0, 3.0, 4.0, 6.0, -0.0, -0.5, -1.0, -1.5, -2.0, -3.0, -4.0, -6.0])


def pack_weight(w, fmt):
    k, n = w.shape
    w = f64(bf(w)).reshape(k // 32, 32, n)
    amax = np.abs(w).max(1)
    if fmt == "e4m3":
        byte = np.frexp(amax)[1] - 1 + 127 - 7
    else:
        mant, ex = np.frexp(amax / 6.0)
        byte = np.where(mant > 0.5, ex, ex - 1) + 127
    byte = np.clip(np.where(amax > 0, byte, 1), 1, 254)
    scaled = (w * np.exp2(127.0 - byte)[:, None, :]).reshape(k, n).astype(np.float32)
    by_word = np.ascontiguousarray(scaled.reshape(k // 512, 128, 4, n).transpose(0, 1, 3, 2))
    if fmt == "e4m3":
        words = by_word.astype(ml_dtypes.float8_e4m3fn).view(np.uint8)
    else:
        c = by_word.astype(ml_dtypes.float4_e2m1fn).view(np.uint8) & 0xF
        words = c[..., 0::2] | (c[..., 1::2] << 4)
    return np.ascontiguousarray(words), np.ascontiguousarray(byte.astype(np.uint8).reshape(k // 512, 16, n))


def unpack_weight(words, scales, fmt):
    g, p, n, _ = words.shape
    if fmt == "e4m3":
        vals = np.ascontiguousarray(words).view(ml_dtypes.float8_e4m3fn).astype(np.float64)
    else:
        nib = np.empty((g, p, n, 4), np.uint8)
        nib[..., 0::2] = words & 0xF
        nib[..., 1::2] = words >> 4
        vals = E2M1[nib]
    vals = vals * np.repeat(np.exp2(scales.astype(np.float64) - 127.0), 8, axis=1)[..., None]
    return vals.transpose(0, 1, 3, 2).reshape(g * 512, n)
def pack4(w):
    words, scales = pack_weight(w, "e2m1")
    return words.reshape(words.shape[0], 128, -1), scales


def unpack4(words, scales):
    return unpack_weight(words.reshape(words.shape[0], 128, -1, 2), scales, "e2m1")


E4M3FN = np.array([(-1.0 if i & 128 else 1.0) * ((1.0 + (i & 7) / 8.0) * 2.0 ** (((i >> 3) & 15) - 7) if i & 120 else (i & 7) * 2.0 ** -9) for i in range(256)])


def e4m3fn_bytes(y):
    return np.clip(np.asarray(y, np.float64), -448.0, 448.0).astype(np.float32).astype(ml_dtypes.float8_e4m3fn).view(np.uint8)


def e4m3fn_values(b):
    return E4M3FN[b]


K, N, B = 1024, 1024, 1024

C_LOGISTIC = 1.702
T_STEP = 0.8


def sigmoid(v):
    return 1.0 / (1.0 + np.exp(-v))


def relu(v):
    return np.maximum(v, 0.0)


def interval_score(z, lo, up):
    c = C_LOGISTIC
    return c * (sigmoid(c * (up - z)) + sigmoid(c * (lo - z)) - 1.0)


def pam4_staircase(q):
    t = T_STEP
    total = np.zeros_like(q)
    for tau in (-2.0, 0.0, 2.0):
        total = total + (relu(q - tau + t) - relu(q - tau - t))
    return -3.0 + (1.0 / t) * total


def draw0():
    s, u = mx_kscale(K), mx_kscale(N)
    inputs = {
        "x": bf(1.5 * np.random.standard_normal((K, B))),
        "p": bf((1.0 + 0.2 * np.random.standard_normal(K)) * s),
        "h": bf(0.7 * np.random.standard_normal((N, K)) / np.sqrt(K) / s[None, :]),
        "lo": bf(np.random.standard_normal((N, B))),
        "width": bf(np.random.uniform(0.5, 1.5, (N, B))),
        "g": bf((1.0 + 0.2 * np.random.standard_normal(N)) * u),
    }
    w = np.random.standard_normal((K, N)) / np.sqrt(N) / u[None, :]
    words, scales = pack4(w.T)
    inputs["w_words"] = words
    inputs["w_scales"] = scales
    return inputs


def core(x, p, h, lo, width, g, w_words, w_scales):
    x, p, h, lo, width, g = f64(x), f64(p), f64(h), f64(lo), f64(width), f64(g)
    z = mxq(h, 1, "e4m3") @ mxq(p[:, None] * x, 0, "e4m3")
    up = lo + width
    r = interval_score(z, lo, up)
    d = unpack4(w_words, w_scales).T @ mxq(g[:, None] * r, 0, "e4m3")
    q = x + d
    return pam4_staircase(q)


def setup_inputs():
    drawn = draw0()
    full = np.asarray(drawn['h']).astype(np.float64)
    scale = (np.abs(full).reshape(1024, 8, 128).max(axis=(2,)) / 448.0).astype(np.float32)
    given = {}
    for key, value in drawn.items():
        if key == 'h':
            given['h_bytes'] = e4m3fn_bytes(full / np.repeat(scale.astype(np.float64), 128, axis=1))
            given['h_scale'] = scale
        else:
            given[key] = value
    return given


def reference(x, p, h_bytes, h_scale, lo, width, g, w_words, w_scales):
    return core(x, p, e4m3fn_values(h_bytes) * np.repeat(h_scale.astype(np.float64), 128, axis=1), lo, width, g, w_words, w_scales)

@@ -1,0 +1,492 @@
+from contextlib import ExitStack
+
+import concourse.mybir as mybir
+from concourse.masks import make_identity
+
+SIZE = 1024
+P = 128
+CW = [256, 256, 256, 128, 128]
+C0 = [0, 256, 512, 768, 896]
+CHUNKS = len(CW)
+C_LOGISTIC = 1.702
+FLOPS = 4 * SIZE * SIZE * SIZE
+
+F32 = mybir.dt.float32
+BF16 = mybir.dt.bfloat16
+U32 = mybir.dt.uint32
+I32 = mybir.dt.int32
+U8 = mybir.dt.uint8
+FP8 = mybir.dt.float8_e4m3fn
+FP8X4 = mybir.dt.float8_e4m3fn_x4
+FP4X4 = mybir.dt.float4_e2m1fn_x4
+ADD = mybir.AluOpType.add
+SUB = mybir.AluOpType.subtract
+MUL = mybir.AluOpType.mult
+MAX = mybir.AluOpType.max
+MIN = mybir.AluOpType.min
+ACT = mybir.ActivationFunctionType
+
+
+def tile_fewbitadclogisticscoreunfoldedstep_d1p_kernel(
+    tc, x, p, h_bytes, h_scale, lo, width, g, w_words, w_scales, out
+):
+    nc = tc.nc
+    with ExitStack() as ctx:
+        keep = ctx.enter_context(tc.tile_pool(name="keep", bufs=1))
+        work = ctx.enter_context(tc.tile_pool(name="work", bufs=2))
+        psum = ctx.enter_context(tc.psum_pool(name="psum", bufs=2))
+        ctx.enter_context(tc.manual_schedule())
+
+        x_v = x.rearrange("(g p t) b -> g p t b", p=P, t=4)
+        lo_v = lo.rearrange("(g p t) b -> g p t b", p=P, t=4)
+        wd_v = width.rearrange("(g p t) b -> g p t b", p=P, t=4)
+        h_v = h_bytes.rearrange("(g p t) k -> g p t k", p=P, t=4)
+        out_v = out.rearrange("(g p t) b -> g p t b", p=P, t=4)
+
+        hs = keep.tile([P, 2, 32], F32)
+        p_sb = keep.tile([P, 2, 4], BF16)
+        g_sb = keep.tile([P, 2, 4], BF16)
+        hb = {}
+        for gg in range(2):
+            for tp in range(2):
+                hb_t = keep.tile([P, 2, SIZE], U8, name=f"hb{gg}{tp}")
+                hb[(gg, tp)] = hb_t
+        xs, los, wds = {}, {}, {}
+
+        def load_planes(store, view, label, gg, c, n):
+            first, total = C0[c], sum(CW[c : c + n])
+            t_sb = keep.tile([P, 4, total], BF16, name=f"{label}{gg}_{c}")
+            nc.sync.dma_start(out=t_sb[:], in_=view[gg][:, :, first : first + total])
+            for i in range(c, c + n):
+                store[(i, gg)] = t_sb[:, :, C0[i] - first : C0[i] - first + CW[i]]
+
+        def load_h(gg, tp):
+            nc.sync.dma_start(out=hb[(gg, tp)][:], in_=h_v[gg][:, 2 * tp : 2 * tp + 2, :])
+
+        nc.sync.dma_start(out=p_sb[:], in_=p.rearrange("(g p t) -> p g t", p=P, t=4))
+        nc.sync.dma_start(out=hs[:], in_=h_scale.rearrange("(g p t) j -> p g (t j)", p=P, t=4))
+        load_h(0, 0)
+        load_planes(xs, x_v, "x", 0, 0, 1)
+        load_planes(xs, x_v, "x", 1, 0, 1)
+        load_h(0, 1)
+        load_planes(los, lo_v, "lo", 0, 0, 1)
+        load_planes(wds, wd_v, "wd", 0, 0, 1)
+        nc.sync.dma_start(out=g_sb[:], in_=g.rearrange("(g p t) -> p g t", p=P, t=4))
+        load_h(1, 0)
+        load_h(1, 1)
+        load_planes(los, lo_v, "lo", 1, 0, 1)
+        load_planes(wds, wd_v, "wd", 1, 0, 1)
+        load_planes(xs, x_v, "x", 0, 1, 1)
+        load_planes(xs, x_v, "x", 1, 1, 1)
+        for gg in range(2):
+            load_planes(los, lo_v, "lo", gg, 1, 1)
+            load_planes(wds, wd_v, "wd", gg, 1, 1)
+        wt = keep.tile([P, 2, 2 * SIZE], U8, align_bytes=64)
+        ws = keep.tile([P, 2, SIZE], U8, align_bytes=64)
+        nc.gpsimd.memset(ws[:].rearrange("p g n -> p (g n)").bitcast(U32), 0)
+        ws_v = w_scales.bitcast(I32).rearrange("g q n -> q g n")
+        for q in range(4):
+            nc.sync.dma_start(out=ws[32 * q : 32 * q + 4, :, :].bitcast(I32), in_=ws_v[4 * q : 4 * q + 4])
+        for gg in range(2):
+            nc.sync.dma_start(out=wt[:, gg, :].bitcast(I32), in_=w_words[gg].bitcast(I32))
+        for gg in range(2):
+            load_planes(xs, x_v, "x", gg, 2, 3)
+        for gg in range(2):
+            load_planes(los, lo_v, "lo", gg, 2, 3)
+            load_planes(wds, wd_v, "wd", gg, 2, 3)
+
+        ident = keep.tile([P, P], F32)
+        make_identity(nc, ident[:])
+        warm = keep.tile([P, 1], F32)
+        nc.vector.memset(warm[:], 0.0)
+        nc.scalar.activation(out=warm[:], in_=warm[:], func=ACT.Tanh)
+
+        ident_bf = keep.tile([P, P], BF16)
+        nc.vector.tensor_copy(out=ident_bf[:], in_=ident[:])
+        diag = keep.tile([P, 8, P], BF16)
+        gc = keep.tile([P, 2, 4], F32)
+
+        hw, hx, hi, hq = {}, {}, {}, {}
+
+        def widen(rt, vec):
+            gg, t = divmod(rt, 4)
+            hw_t = work.tile([P, SIZE], BF16, bufs=8, align_bytes=64)
+            hw[rt] = hw_t
+            for j in range(8):
+                cols = slice(j * P, (j + 1) * P)
+                src = hb[(gg, t // 2)][:, t % 2, cols].bitcast(FP8)
+                sc = hs[:, gg, t * 8 + j : t * 8 + j + 1]
+                if j in vec:
+                    nc.vector.tensor_scalar(out=hw_t[:, cols], in0=src, scalar1=sc, scalar2=None, op0=MUL)
+                else:
+                    nc.scalar.activation(out=hw_t[:, cols], in_=src, func=ACT.Copy, scale=sc)
+
+        def turn(rt):
+            hx_t = psum.tile([P, 2, 2, P], F32, tag="do"[rt % 2], name=f"hx{rt}")
+            hx[rt] = hx_t
+            words = hw[rt][:].bitcast(F32)
+            for k in range(2):
+                for u in range(2):
+                    nc.tensor.transpose(hx_t[:, k, u, :], words[:, 256 * k + u : 256 * (k + 1) : 2], ident[:])
+
+        def h_copy(rt, vec=True):
+            hi_t = work.tile([P, 2, P, 4], BF16, bufs=4, align_bytes=64)
+            hi[rt] = hi_t
+            move = nc.vector.tensor_copy if vec else nc.scalar.copy
+            move(
+                out=hi_t[:].rearrange("p k r t -> p (k r t)").bitcast(F32).rearrange("p (k r u) -> p k r u", k=2, u=2),
+                in_=hx[rt][:].rearrange("p k u r -> p k r u"),
+            )
+
+        def h_quant(rt):
+            codes = keep.tile([P, 2, P], U32, name=f"hc{rt}", align_bytes=64)
+            scales = keep.tile([P, 2, P], U8, name=f"hsc{rt}", align_bytes=64)
+            hq[rt] = (codes, scales)
+            nc.vector.quantize_mx(
+                out=codes[:].rearrange("p k r -> p (k r)").bitcast(FP8X4),
+                scales=scales[:].rearrange("p k r -> p (k r)"),
+                in_=hi[rt][:].rearrange("p k r t -> p (k r t)"),
+            )
+
+        px, xi, xq = {}, {}, {}
+
+        def px_mm(c, gg):
+            px_t = psum.tile([P, 4, CW[c]], BF16, tag="a", name=f"px{c}{gg}")
+            px[(c, gg)] = px_t
+            for t in range(4):
+                nc.tensor.matmul(px_t[:, t, :], lhsT=diag[:, 4 * gg + t, :], rhs=xs[(c, gg)][:, t, :], start=True, stop=True)
+
+        def px_copy(c, gg, vec=False):
+            xi_t = work.tile([P, CW[c], 4], BF16, bufs=2, align_bytes=64)
+            xi[(c, gg)] = xi_t
+            src = px[(c, gg)][:].rearrange("p t b -> p b t")
+            if vec:
+                nc.vector.tensor_copy(out=xi_t[:], in_=src)
+            else:
+                nc.scalar.copy(out=xi_t[:], in_=src)
+
+        def px_quant(c, gg):
+            codes = work.tile([P, CW[c]], U32, tag=f"xc{gg}", name=f"xc{c}{gg}", bufs=2, align_bytes=64)
+            scales = work.tile([P, CW[c]], U8, tag=f"xsc{gg}", name=f"xsc{c}{gg}", bufs=2, align_bytes=64)
+            xq[(c, gg)] = (codes, scales)
+            nc.vector.quantize_mx(
+                out=codes[:].bitcast(FP8X4), scales=scales[:], in_=xi[(c, gg)][:].rearrange("p b t -> p (b t)")
+            )
+
+        z, a1, a2, t1, rb, ri, rq = {}, {}, {}, {}, {}, {}, {}
+
+        def banks(c):
+            n = 512 // CW[c]
+            return [(t, n) for t in range(0, 4, n)]
+
+        def z_mm(c, gg, t0, n):
+            z_t = psum.tile([P, n, CW[c]], F32, tag="z", name=f"z{c}{gg}{t0}")
+            z[(c, gg, t0)] = z_t
+            for t in range(t0, t0 + n):
+                hc, hsc = hq[4 * gg + t]
+                for k in range(2):
+                    xc, xsc = xq[(c, k)]
+                    nc.tensor.matmul_mx(
+                        out=z_t[:, t - t0, :],
+                        lhsT=hc[:, k, :].bitcast(FP8X4),
+                        lhsT_scale=hsc[:, k, :],
+                        rhs=xc[:].bitcast(FP8X4),
+                        rhs_scale=xsc[:],
+                        start=(k == 0),
+                        stop=(k == 1),
+                    )
+
+        def lo_minus_z(c, gg, t0, n):
+            if t0 == 0:
+                a1_t = work.tile([P, 4, CW[c]], F32, bufs=2)
+                a1[(c, gg)] = a1_t
+            ts = slice(t0, t0 + n)
+            nc.vector.tensor_tensor(out=a1[(c, gg)][:, ts, :], in0=los[(c, gg)][:, ts, :], in1=z[(c, gg, t0)][:], op=SUB)
+
+        def add_width(c, gg):
+            a2_t = work.tile([P, 4, CW[c]], F32, bufs=2)
+            a2[(c, gg)] = a2_t
+            nc.vector.tensor_tensor(out=a2_t[:], in0=a1[(c, gg)][:], in1=wds[(c, gg)], op=ADD)
+
+        def tanh_lo(c, gg):
+            t1_t = work.tile([P, 4, CW[c]], F32, bufs=2)
+            t1[(c, gg)] = t1_t
+            nc.scalar.activation(out=t1_t[:], in_=a1[(c, gg)][:], func=ACT.Tanh, scale=C_LOGISTIC / 2)
+
+        def tanh_up(c, gg):
+            nc.scalar.activation(out=a2[(c, gg)][:], in_=a2[(c, gg)][:], func=ACT.Tanh, scale=C_LOGISTIC / 2)
+
+        def tanh_sum(c, gg):
+            nc.vector.tensor_tensor(out=t1[(c, gg)][:], in0=t1[(c, gg)][:], in1=a2[(c, gg)][:], op=ADD)
+
+        def times_g(c, gg, planes, vec=False):
+            if (c, gg) not in rb:
+                rb_t = work.tile([P, 4, CW[c]], BF16, bufs=2)
+                rb[(c, gg)] = rb_t
+            for t in planes:
+                dst, src, col = rb[(c, gg)][:, t, :], t1[(c, gg)][:, t, :], gc[:, gg, t : t + 1]
+                if vec:
+                    nc.vector.tensor_scalar(out=dst, in0=src, scalar1=col, scalar2=None, op0=MUL)
+                else:
+                    nc.scalar.activation(out=dst, in_=src, func=ACT.Copy, scale=col)
+
+        def r_inter(c, gg, vec=False):
+            ri_t = work.tile([P, 4 * CW[c]], BF16, bufs=2, align_bytes=64)
+            ri[(c, gg)] = ri_t
+            move = nc.vector.tensor_copy if vec else nc.scalar.copy
+            move(
+                out=ri_t[:].rearrange("p (c i t) -> p c t i", i=4, t=4),
+                in_=rb[(c, gg)][:].rearrange("p t (c i) -> p c t i", i=4),
+            )
+
+        def r_quant(c, gg):
+            codes = work.tile([P, CW[c]], U32, tag=f"rc{gg}", name=f"rc{c}{gg}", bufs=2, align_bytes=64)
+            scales = work.tile([P, CW[c]], U8, tag=f"rsc{gg}", name=f"rsc{c}{gg}", bufs=2, align_bytes=64)
+            rq[(c, gg)] = (codes, scales)
+            nc.vector.quantize_mx(out=codes[:].bitcast(FP8X4), scales=scales[:], in_=ri[(c, gg)][:])
+
+        d, xtp, xt, q, cl, op = {}, {}, {}, {}, {}, {}
+
+        def where(e):
+            c = max(i for i in range(CHUNKS) if C0[i] <= e * P)
+            return c, slice(e * P - C0[c], (e + 1) * P - C0[c])
+
+        def d_mm(e):
+            c, cols = where(e)
+            for kh in range(2):
+                d_t = psum.tile([P, 512], F32, tag="d", name=f"d{e}{kh}")
+                d[(e, kh)] = d_t
+                for k in range(2):
+                    rc, rsc = rq[(c, k)]
+                    nc.tensor.matmul_mx(
+                        out=d_t[:],
+                        lhsT=rc[:, cols].bitcast(FP8X4),
+                        lhsT_scale=rsc[:, cols],
+                        rhs=wt[:, k, 1024 * kh : 1024 * (kh + 1)].bitcast(FP4X4),
+                        rhs_scale=ws[:, k, 512 * kh : 512 * (kh + 1)],
+                        start=(k == 0),
+                        stop=(k == 1),
+                    )
+
+        def x_turn(e):
+            c, cols = where(e)
+            xtp_t = psum.tile([P, 2, 4, P], BF16, tag="a", name=f"xtp{e}")
+            xtp[e] = xtp_t
+            for kh in range(2):
+                for t in range(4):
+                    nc.tensor.transpose(xtp_t[:, kh, t, :], xs[(c, kh)][:, t, cols], ident_bf[:])
+
+        def x_turn_copy(e, vec=False):
+            xt_t = work.tile([P, 2, 4, P], BF16, bufs=3)
+            xt[e] = xt_t
+            move = nc.vector.tensor_copy if vec else nc.scalar.copy
+            move(out=xt_t[:], in_=xtp[e][:])
+
+        def q_sum(e, kh):
+            if kh == 0:
+                q_t = work.tile([P, 2, 4, P], F32, bufs=2)
+                q[e] = q_t
+            nc.vector.tensor_tensor(
+                out=q[e][:, kh], in0=d[(e, kh)][:].rearrange("b (s t) -> b t s", t=4), in1=xt[e][:, kh], op=ADD
+            )
+
+        def clip(e, i, halves=(slice(0, 2),)):
+            if i == 0:
+                if e not in cl:
+                    cl[e] = {}
+            if i not in cl[e]:
+                cl_t = work.tile([P, 2, 4, P], F32, tag=f"cl{i}", name=f"cl{e}{i}", bufs=2)
+                cl[e][i] = cl_t
+            low = 2.0 * i - 2.8
+            for s in halves:
+                nc.vector.tensor_scalar(
+                    out=cl[e][i][:, s], in0=q[e][:, s], scalar1=low, scalar2=low + 1.6, op0=MAX, op1=MIN
+                )
+
+        def out_turn(e, kh):
+            op_t = psum.tile([P, 4, P], F32, tag="o", name=f"o{e}{kh}")
+            op[(e, kh)] = op_t
+            for t in range(4):
+                for i in range(3):
+                    nc.tensor.matmul(
+                        op_t[:, t, :],
+                        lhsT=cl[e][i][:, kh, t, :],
+                        rhs=ident[:],
+                        is_transpose=True,
+                        start=(i == 0),
+                        stop=(i == 2),
+                    )
+
+        def out_copy(e, kh, vec=False):
+            ot_t = work.tile([P, 4, P], F32, bufs=4)
+            if vec:
+                nc.vector.tensor_scalar(out=ot_t[:], in0=op[(e, kh)][:], scalar1=1.25, scalar2=None, op0=MUL)
+            else:
+                nc.scalar.activation(out=ot_t[:], in_=op[(e, kh)][:], func=ACT.Copy, scale=1.25)
+            nc.sync.dma_start(out=out_v[kh][:, :, e * P : (e + 1) * P], in_=ot_t[:])
+
+        GCV = {}
+        ILV = [(0, 0), (0, 1)]
+        ALL = range(8)
+        for i in range(8):
+            nc.vector.tensor_scalar(
+                out=diag[:, i, :], in0=ident[:], scalar1=p_sb[:, i // 4, i % 4 : i % 4 + 1], scalar2=None, op0=MUL
+            )
+        widen(0, range(4))
+        turn(0)
+        widen(1, range(4))
+        px_mm(0, 0)
+        px_copy(0, 0)
+        px_mm(0, 1)
+        turn(1)
+        widen(3, range(6))
+        h_copy(0)
+        px_copy(0, 1, vec=True)
+        h_copy(1)
+        widen(2, ())
+        turn(3)
+        turn(2)
+        h_quant(0)
+        h_quant(1)
+        h_copy(3)
+        px_quant(0, 0)
+        px_quant(0, 1)
+        z_mm(0, 0, 0, 2)
+        h_copy(2)
+        h_quant(3)
+        h_quant(2)
+        widen(4, ())
+        turn(4)
+        widen(5, ())
+        turn(5)
+        nc.vector.tensor_scalar(out=gc[:], in0=g_sb[:], scalar1=C_LOGISTIC / 2, scalar2=None, op0=MUL)
+        lo_minus_z(0, 0, 0, 2)
+        z_mm(0, 0, 2, 2)
+        px_mm(1, 0)
+        h_copy(4)
+        h_copy(5)
+        lo_minus_z(0, 0, 2, 2)
+        widen(6, ())
+        turn(6)
+        tanh_lo(0, 0)
+        widen(7, ())
+        turn(7)
+        h_quant(4)
+        h_quant(5)
+        z_mm(0, 1, 0, 2)
+        px_mm(1, 1)
+        add_width(0, 0)
+        px_copy(1, 0)
+        tanh_up(0, 0)
+        h_copy(6)
+        lo_minus_z(0, 1, 0, 2)
+        h_copy(7)
+        px_copy(1, 1)
+        h_quant(6)
+        h_quant(7)
+        z_mm(0, 1, 2, 2)
+        px_quant(1, 0)
+        lo_minus_z(0, 1, 2, 2)
+        tanh_lo(0, 1)
+        px_quant(1, 1)
+        for t0, n in banks(1):
+            z_mm(1, 0, t0, n)
+        add_width(0, 1)
+        tanh_up(0, 1)
+
+        tiles = [[e for e in range(8) if where(e)[0] == c] for c in range(CHUNKS)]
+        for c in range(1, CHUNKS + 2):
+            prev, nxt = c - 1, c + 1
+            es = tiles[c - 2] if c >= 2 else []
+            es_next = tiles[c - 1] if c - 1 < CHUNKS else []
+            has_c, has_prev, has_next = c < CHUNKS, prev < CHUNKS, nxt < CHUNKS
+            gv = [GCV.get((prev, gg), 2) for gg in range(2)]
+            if has_next:
+                px_mm(nxt, 0)
+            if has_next:
+                px_mm(nxt, 1)
+                px_copy(nxt, 0)
+            if has_prev:
+                tanh_sum(prev, 0)
+                times_g(prev, 0, range(4 - gv[0]))
+            if has_c:
+                for t0, n in banks(c):
+                    lo_minus_z(c, 0, t0, n)
+                for t0, n in banks(c):
+                    z_mm(c, 1, t0, n)
+            if has_prev:
+                tanh_sum(prev, 1)
+                times_g(prev, 0, range(4 - gv[0], 4), vec=True)
+                r_inter(prev, 0, vec=(prev, 0) in ILV)
+                times_g(prev, 1, range(4 - gv[1]))
+            if es:
+                q_sum(es[0], 0)
+                q_sum(es[0], 1)
+            if len(es) == 2:
+                d_mm(es[1])
+            if has_next:
+                px_copy(nxt, 1)
+            for e in es_next:
+                x_turn(e)
+            if has_c:
+                for t0, n in banks(c):
+                    lo_minus_z(c, 1, t0, n)
+                tanh_lo(c, 0)
+            if es:
+                clip(es[0], 0)
+            if has_prev:
+                times_g(prev, 1, range(4 - gv[1], 4), vec=True)
+            if es:
+                clip(es[0], 1)
+            if has_prev:
+                r_inter(prev, 1, vec=(prev, 1) in ILV)
+            if has_c:
+                add_width(c, 0)
+            if es:
+                clip(es[0], 2)
+                if has_c:
+                    out_turn(es[0], 0)
+                    out_turn(es[0], 1)
+            if has_c:
+                tanh_up(c, 0)
+            for e in es_next:
+                x_turn_copy(e)
+            if has_prev:
+                r_quant(prev, 0)
+            if len(es) == 2:
+                q_sum(es[1], 0)
+                q_sum(es[1], 1)
+            if es and has_c:
+                out_copy(es[0], 0)
+                out_copy(es[0], 1)
+            if has_c:
+                add_width(c, 1)
+                tanh_lo(c, 1)
+                tanh_up(c, 1)
+            if has_next:
+                px_quant(nxt, 0)
+            if len(es) == 2:
+                clip(es[1], 0)
+            if has_prev:
+                r_quant(prev, 1)
+            if len(es) == 2:
+                clip(es[1], 1)
+            if has_next:
+                px_quant(nxt, 1)
+            if len(es) == 2:
+                clip(es[1], 2)
+            if es_next:
+                d_mm(es_next[0])
+            if es and not has_c:
+                out_turn(es[0], 0)
+                out_turn(es[0], 1)
+                out_copy(es[0], 0)
+                out_copy(es[0], 1)
+            if has_next:
+                for t0, n in banks(nxt):
+                    z_mm(nxt, 0, t0, n)
+            if len(es) == 2:
+                out_turn(es[1], 0)
+                out_turn(es[1], 1)
+                out_copy(es[1], 0)
+                out_copy(es[1], 1)

@@ -157,7 +157,7 @@ def tile_fewbitadclogisticscoreunfoldedstep_d1p_kernel(
                 nc.tensor.matmul(px_t[:, t, :], lhsT=diag[:, 4 * gg + t, :], rhs=xs[(c, gg)][:, t, :], start=True, stop=True)
 
         def px_copy(c, gg, vec=False):
-            xi_t = work.tile([P, CW[c], 4], BF16, bufs=2, align_bytes=64)
+            xi_t = work.tile([P, CW[c], 4], BF16, bufs=3, align_bytes=64)
             xi[(c, gg)] = xi_t
             src = px[(c, gg)][:].rearrange("p t b -> p b t")
             if vec:
@@ -166,8 +166,8 @@ def tile_fewbitadclogisticscoreunfoldedstep_d1p_kernel(
                 nc.scalar.copy(out=xi_t[:], in_=src)
 
         def px_quant(c, gg):
-            codes = work.tile([P, CW[c]], U32, tag=f"xc{gg}", name=f"xc{c}{gg}", bufs=2, align_bytes=64)
-            scales = work.tile([P, CW[c]], U8, tag=f"xsc{gg}", name=f"xsc{c}{gg}", bufs=2, align_bytes=64)
+            codes = work.tile([P, CW[c]], U32, tag=f"xc{gg}", name=f"xc{c}{gg}", bufs=3, align_bytes=64)
+            scales = work.tile([P, CW[c]], U8, tag=f"xsc{gg}", name=f"xsc{c}{gg}", bufs=3, align_bytes=64)
             xq[(c, gg)] = (codes, scales)
             nc.vector.quantize_mx(
                 out=codes[:].bitcast(FP8X4), scales=scales[:], in_=xi[(c, gg)][:].rearrange("p b t -> p (b t)")
@@ -179,9 +179,23 @@ def tile_fewbitadclogisticscoreunfoldedstep_d1p_kernel(
             n = 512 // CW[c]
             return [(t, n) for t in range(0, 4, n)]
 
+        def busy(bank, count):
+            for i in range(count):
+                nc.tensor.matmul_mx(
+                    out=bank,
+                    lhsT=hq[0][0][:, 0, :].bitcast(FP8X4),
+                    lhsT_scale=hq[0][1][:, 0, :],
+                    rhs=wt[:, 0, :1024].bitcast(FP4X4),
+                    rhs_scale=ws[:, 0, :512],
+                    start=True,
+                    stop=True,
+                )
+
         def z_mm(c, gg, t0, n):
             z_t = psum.tile([P, n, CW[c]], F32, tag="z", name=f"z{c}{gg}{t0}")
             z[(c, gg, t0)] = z_t
+            if c > 1:
+                busy(z_t[:].rearrange("p t b -> p (t b)"), KN["bz"])
             for t in range(t0, t0 + n):
                 hc, hsc = hq[4 * gg + t]
                 for k in range(2):
@@ -198,18 +212,19 @@ def tile_fewbitadclogisticscoreunfoldedstep_d1p_kernel(
 
         def lo_minus_z(c, gg, t0, n):
             if t0 == 0:
-                a1_t = work.tile([P, 4, CW[c]], F32, bufs=2)
+                a1_t = work.tile([P, 4, CW[c]], F32, bufs=4)
                 a1[(c, gg)] = a1_t
             ts = slice(t0, t0 + n)
             nc.vector.tensor_tensor(out=a1[(c, gg)][:, ts, :], in0=los[(c, gg)][:, ts, :], in1=z[(c, gg, t0)][:], op=SUB)
 
         def add_width(c, gg):
-            a2_t = work.tile([P, 4, CW[c]], F32, bufs=2)
+            a2_t = work.tile([P, 4, CW[c]], F32, bufs=3)
             a2[(c, gg)] = a2_t
-            nc.vector.tensor_tensor(out=a2_t[:], in0=a1[(c, gg)][:], in1=wds[(c, gg)], op=ADD)
+            adder = nc.gpsimd if (c, gg) in KN["a2g"] else nc.vector
+            adder.tensor_tensor(out=a2_t[:], in0=a1[(c, gg)][:], in1=wds[(c, gg)], op=ADD)
 
         def tanh_lo(c, gg):
-            t1_t = work.tile([P, 4, CW[c]], F32, bufs=2)
+            t1_t = work.tile([P, 4, CW[c]], F32, bufs=3)
             t1[(c, gg)] = t1_t
             nc.scalar.activation(out=t1_t[:], in_=a1[(c, gg)][:], func=ACT.Tanh, scale=C_LOGISTIC / 2)
 
@@ -221,7 +236,7 @@ def tile_fewbitadclogisticscoreunfoldedstep_d1p_kernel(
 
         def times_g(c, gg, planes, vec=False):
             if (c, gg) not in rb:
-                rb_t = work.tile([P, 4, CW[c]], BF16, bufs=2)
+                rb_t = work.tile([P, 4, CW[c]], BF16, bufs=3)
                 rb[(c, gg)] = rb_t
             for t in planes:
                 dst, src, col = rb[(c, gg)][:, t, :], t1[(c, gg)][:, t, :], gc[:, gg, t : t + 1]
@@ -231,7 +246,7 @@ def tile_fewbitadclogisticscoreunfoldedstep_d1p_kernel(
                     nc.scalar.activation(out=dst, in_=src, func=ACT.Copy, scale=col)
 
         def r_inter(c, gg, vec=False):
-            ri_t = work.tile([P, 4 * CW[c]], BF16, bufs=2, align_bytes=64)
+            ri_t = work.tile([P, 4 * CW[c]], BF16, bufs=3, align_bytes=64)
             ri[(c, gg)] = ri_t
             move = nc.vector.tensor_copy if vec else nc.scalar.copy
             move(
@@ -256,6 +271,7 @@ def tile_fewbitadclogisticscoreunfoldedstep_d1p_kernel(
             for kh in range(2):
                 d_t = psum.tile([P, 512], F32, tag="d", name=f"d{e}{kh}")
                 d[(e, kh)] = d_t
+                busy(d_t[:], KN["bd"])
                 for k in range(2):
                     rc, rsc = rq[(c, k)]
                     nc.tensor.matmul_mx(
@@ -284,7 +300,7 @@ def tile_fewbitadclogisticscoreunfoldedstep_d1p_kernel(
 
         def q_sum(e, kh):
             if kh == 0:
-                q_t = work.tile([P, 2, 4, P], F32, bufs=2)
+                q_t = work.tile([P, 2, 4, P], F32, bufs=3)
                 q[e] = q_t
             nc.vector.tensor_tensor(
                 out=q[e][:, kh], in0=d[(e, kh)][:].rearrange("b (s t) -> b t s", t=4), in1=xt[e][:, kh], op=ADD
@@ -295,17 +311,19 @@ def tile_fewbitadclogisticscoreunfoldedstep_d1p_kernel(
                 if e not in cl:
                     cl[e] = {}
             if i not in cl[e]:
-                cl_t = work.tile([P, 2, 4, P], F32, tag=f"cl{i}", name=f"cl{e}{i}", bufs=2)
+                cl_t = work.tile([P, 2, 4, P], F32, tag=f"cl{i}", name=f"cl{e}{i}", bufs=3)
                 cl[e][i] = cl_t
             low = 2.0 * i - 2.8
             for s in halves:
-                nc.vector.tensor_scalar(
+                engine = nc.gpsimd if (e, i) in KN["gp"] else nc.vector
+                engine.tensor_scalar(
                     out=cl[e][i][:, s], in0=q[e][:, s], scalar1=low, scalar2=low + 1.6, op0=MAX, op1=MIN
                 )
 
         def out_turn(e, kh):
             op_t = psum.tile([P, 4, P], F32, tag="o", name=f"o{e}{kh}")
             op[(e, kh)] = op_t
+            busy(op_t[:].rearrange("p t b -> p (t b)"), KN["bo"])
             for t in range(4):
                 for i in range(3):
                     nc.tensor.matmul(
@@ -325,168 +343,129 @@ def tile_fewbitadclogisticscoreunfoldedstep_d1p_kernel(
                 nc.scalar.activation(out=ot_t[:], in_=op[(e, kh)][:], func=ACT.Copy, scale=1.25)
             nc.sync.dma_start(out=out_v[kh][:, :, e * P : (e + 1) * P], in_=ot_t[:])
 
-        GCV = {}
-        ILV = [(0, 0), (0, 1)]
-        ALL = range(8)
-        for i in range(8):
-            nc.vector.tensor_scalar(
-                out=diag[:, i, :], in0=ident[:], scalar1=p_sb[:, i // 4, i % 4 : i % 4 + 1], scalar2=None, op0=MUL
-            )
-        widen(0, range(4))
-        turn(0)
-        widen(1, range(4))
-        px_mm(0, 0)
-        px_copy(0, 0)
-        px_mm(0, 1)
-        turn(1)
-        widen(3, range(6))
-        h_copy(0)
-        px_copy(0, 1, vec=True)
-        h_copy(1)
-        widen(2, ())
-        turn(3)
-        turn(2)
-        h_quant(0)
-        h_quant(1)
-        h_copy(3)
-        px_quant(0, 0)
-        px_quant(0, 1)
-        z_mm(0, 0, 0, 2)
-        h_copy(2)
-        h_quant(3)
-        h_quant(2)
-        widen(4, ())
-        turn(4)
-        widen(5, ())
-        turn(5)
-        nc.vector.tensor_scalar(out=gc[:], in0=g_sb[:], scalar1=C_LOGISTIC / 2, scalar2=None, op0=MUL)
-        lo_minus_z(0, 0, 0, 2)
-        z_mm(0, 0, 2, 2)
-        px_mm(1, 0)
-        h_copy(4)
-        h_copy(5)
-        lo_minus_z(0, 0, 2, 2)
-        widen(6, ())
-        turn(6)
-        tanh_lo(0, 0)
-        widen(7, ())
-        turn(7)
-        h_quant(4)
-        h_quant(5)
-        z_mm(0, 1, 0, 2)
-        px_mm(1, 1)
-        add_width(0, 0)
-        px_copy(1, 0)
-        tanh_up(0, 0)
-        h_copy(6)
-        lo_minus_z(0, 1, 0, 2)
-        h_copy(7)
-        px_copy(1, 1)
-        h_quant(6)
-        h_quant(7)
-        z_mm(0, 1, 2, 2)
-        px_quant(1, 0)
-        lo_minus_z(0, 1, 2, 2)
-        tanh_lo(0, 1)
-        px_quant(1, 1)
-        for t0, n in banks(1):
-            z_mm(1, 0, t0, n)
-        add_width(0, 1)
-        tanh_up(0, 1)
-
+        HEAD = "DI WD0 WD2 PX00 WD3 PX01 WD1 TR3 WD4 XC00 TR1 TR0 HC1 TR2 PX10 WD5 HC3 WD7 HQ1 TR5 HQ3 HC5 XC01 PX11 XQ00 TR7 GC XC10 HC2 HQ2 HC0 TR4 HC7 HQ0 XQ01 HQ5 ZZ000 ZZ001 WD6 A1000 HC4 A1001 HQ4 XC11 HQ7 TR6 XQ11 HC6 ZZ010 HQ6 ZZ011 T10 A1010 A20 XQ10 ZZ100 A1011 ZZ101 T11 A1100 A21 A1101 PX20 PX21 T20 T21 ZZ110 ZZ111".split()
+        STEP = "SU0 XC0 Pb0 XC1 Qa0 Qa1 GS0 SU1 Xb Db Ca0 GV0 Ca2 GV1 XQ0 A1 GS1 Xa XQ1 Pb1 Ca1 Yb AW0 IL0 Qb0 Oa1 AW1 IL1 TL0 QR0 Qb1 Pa1 QR1 Cb0 Oa0 Cb2 Ya Cb1 PX1 TU0 Z0 PX0 Da Ob0 TU1 A0 Z1 TL1 Pa0 Ob1".split()
+        TAIL = {5: "Yb SU0 GV0 Ob0 Cb0 SU1 GS0 IL0 Qa0 GV1 Qa1 Qb1 QR0 Ca0 GS1 Xa Pb0 IL1 QR1 Ca1 Qb0 Pb1 Ya Cb1 Da Ca2 Oa1 Oa0 Pa1 Xb Ob1 Cb2 Pa0 Db".split(), 6: "Qa0 Ea0 Ea2 Qa1 Ea4 Ea1 Ea3 Oa0 Ea5 Pa0 Oa1 Pa1".split()}
+        KN = {"wv": {0: [0,1], 1: [0,1,2,3], 2: [0,1,2,3,4,5,6,7], 3: [], 4: [0,1], 5: [], 6: [0,1], 7: [0,1]}, "hcs": [0,1,2,4,5,6,7], "xcv": ["00","01","10"], "gv": {(1, 0): 1, (0, 0): 4, (0, 1): 3, (4, 0): 3, (3, 1): 0, (3, 0): 3, (4, 1): 2, (2, 1): 0, (2, 0): 3, (1, 1): 0}, "ilv": ((0, 1), ), "gp": (), "a2g": (), "bo": 0, "bd": 0, "bz": 0}
+        outs = []
         tiles = [[e for e in range(8) if where(e)[0] == c] for c in range(CHUNKS)]
-        for c in range(1, CHUNKS + 2):
+        late = {}
+
+        def head_token(tok):
+            name, arg = tok[:2], tok[2:]
+            if name == "WD":
+                widen(int(arg), KN["wv"][int(arg)])
+            elif name == "TR":
+                turn(int(arg))
+            elif name == "HC":
+                h_copy(int(arg), vec=int(arg) not in KN["hcs"])
+            elif name == "HQ":
+                h_quant(int(arg))
+            elif name == "PX":
+                px_mm(int(arg[0]), int(arg[1]))
+            elif name == "XC":
+                px_copy(int(arg[0]), int(arg[1]), vec=arg in KN["xcv"])
+            elif name == "XQ":
+                px_quant(int(arg[0]), int(arg[1]))
+            elif name == "ZZ":
+                t0, n = banks(int(arg[0]))[int(arg[2])]
+                z_mm(int(arg[0]), int(arg[1]), t0, n)
+            elif name == "A1":
+                t0, n = banks(int(arg[0]))[int(arg[2])]
+                lo_minus_z(int(arg[0]), int(arg[1]), t0, n)
+            elif name == "A2":
+                add_width(0, int(arg))
+            elif name == "T1":
+                tanh_lo(0, int(arg))
+            elif name == "T2":
+                tanh_up(0, int(arg))
+            elif name == "GC":
+                nc.vector.tensor_scalar(out=gc[:], in0=g_sb[:], scalar1=C_LOGISTIC / 2, scalar2=None, op0=MUL)
+            elif name == "DI":
+                for i in range(8):
+                    nc.vector.tensor_scalar(
+                        out=diag[:, i, :], in0=ident[:], scalar1=p_sb[:, i // 4, i % 4 : i % 4 + 1], scalar2=None, op0=MUL
+                    )
+            else:
+                raise ValueError(tok)
+
+        def step_token(tok, c):
             prev, nxt = c - 1, c + 1
-            es = tiles[c - 2] if c >= 2 else []
-            es_next = tiles[c - 1] if c - 1 < CHUNKS else []
-            has_c, has_prev, has_next = c < CHUNKS, prev < CHUNKS, nxt < CHUNKS
-            gv = [GCV.get((prev, gg), 2) for gg in range(2)]
-            if has_next:
-                px_mm(nxt, 0)
-            if has_next:
-                px_mm(nxt, 1)
-                px_copy(nxt, 0)
-            if has_prev:
-                tanh_sum(prev, 0)
-                times_g(prev, 0, range(4 - gv[0]))
-            if has_c:
-                for t0, n in banks(c):
-                    lo_minus_z(c, 0, t0, n)
-                for t0, n in banks(c):
-                    z_mm(c, 1, t0, n)
-            if has_prev:
-                tanh_sum(prev, 1)
-                times_g(prev, 0, range(4 - gv[0], 4), vec=True)
-                r_inter(prev, 0, vec=(prev, 0) in ILV)
-                times_g(prev, 1, range(4 - gv[1]))
-            if es:
-                q_sum(es[0], 0)
-                q_sum(es[0], 1)
-            if len(es) == 2:
-                d_mm(es[1])
-            if has_next:
-                px_copy(nxt, 1)
-            for e in es_next:
-                x_turn(e)
-            if has_c:
-                for t0, n in banks(c):
-                    lo_minus_z(c, 1, t0, n)
-                tanh_lo(c, 0)
-            if es:
-                clip(es[0], 0)
-            if has_prev:
-                times_g(prev, 1, range(4 - gv[1], 4), vec=True)
-            if es:
-                clip(es[0], 1)
-            if has_prev:
-                r_inter(prev, 1, vec=(prev, 1) in ILV)
-            if has_c:
-                add_width(c, 0)
-            if es:
-                clip(es[0], 2)
-                if has_c:
-                    out_turn(es[0], 0)
-                    out_turn(es[0], 1)
-            if has_c:
-                tanh_up(c, 0)
-            for e in es_next:
-                x_turn_copy(e)
-            if has_prev:
-                r_quant(prev, 0)
-            if len(es) == 2:
-                q_sum(es[1], 0)
-                q_sum(es[1], 1)
-            if es and has_c:
-                out_copy(es[0], 0)
-                out_copy(es[0], 1)
-            if has_c:
-                add_width(c, 1)
-                tanh_lo(c, 1)
-                tanh_up(c, 1)
-            if has_next:
-                px_quant(nxt, 0)
-            if len(es) == 2:
-                clip(es[1], 0)
-            if has_prev:
-                r_quant(prev, 1)
-            if len(es) == 2:
-                clip(es[1], 1)
-            if has_next:
-                px_quant(nxt, 1)
-            if len(es) == 2:
-                clip(es[1], 2)
-            if es_next:
-                d_mm(es_next[0])
-            if es and not has_c:
-                out_turn(es[0], 0)
-                out_turn(es[0], 1)
-                out_copy(es[0], 0)
-                out_copy(es[0], 1)
-            if has_next:
+            es = tiles[c - 2] if 2 <= c < CHUNKS + 2 else []
+            en = tiles[c - 1] if c - 1 < CHUNKS else []
+            before = tiles[c - 3] if c >= 3 else []
+            has_c, has_p, has_n = c < CHUNKS, prev < CHUNKS, nxt < CHUNKS
+            ea, eb = (es[0] if es else None), (es[1] if len(es) == 2 else None)
+            na, nb = (en[0] if en else None), (en[1] if len(en) == 2 else None)
+            lt = before[1] if len(before) == 2 else None
+            name, arg = tok[:2], (int(tok[2]) if len(tok) > 2 else 0)
+            if name == "SU" and has_p:
+                tanh_sum(prev, arg)
+            elif name == "GS" and has_p:
+                times_g(prev, arg, range(4 - KN["gv"].get((prev, arg), 2)))
+            elif name == "GV" and has_p:
+                times_g(prev, arg, range(4 - KN["gv"].get((prev, arg), 2), 4), vec=True)
+            elif name == "IL" and has_p:
+                r_inter(prev, arg, vec=(prev, arg) in KN["ilv"])
+            elif name == "QR" and has_p:
+                r_quant(prev, arg)
+            elif name == "XC" and has_n:
+                px_copy(nxt, arg, vec=str(nxt) + str(arg) in KN["xcv"])
+            elif name == "XQ" and has_n:
+                px_quant(nxt, arg)
+            elif name == "PX" and c + 2 < CHUNKS:
+                px_mm(c + 2, arg)
+            elif name == "Z0" and has_n:
                 for t0, n in banks(nxt):
                     z_mm(nxt, 0, t0, n)
-            if len(es) == 2:
-                out_turn(es[1], 0)
-                out_turn(es[1], 1)
-                out_copy(es[1], 0)
-                out_copy(es[1], 1)
+            elif name == "Z1" and has_n:
+                for t0, n in banks(nxt):
+                    z_mm(nxt, 1, t0, n)
+            elif name == "A0" and has_n:
+                for t0, n in banks(nxt):
+                    lo_minus_z(nxt, 0, t0, n)
+            elif name == "A1" and has_c:
+                for t0, n in banks(c):
+                    lo_minus_z(c, 1, t0, n)
+            elif name == "AW" and has_c:
+                add_width(c, arg)
+            elif name == "TL" and has_c:
+                tanh_lo(c, arg)
+            elif name == "TU" and has_c:
+                tanh_up(c, arg)
+            elif name == "Da" and na is not None:
+                d_mm(na)
+            elif name == "Db" and eb is not None:
+                d_mm(eb)
+            elif name == "Qa" and ea is not None:
+                q_sum(ea, arg)
+            elif name == "Qb" and eb is not None:
+                q_sum(eb, arg)
+            elif name == "Ca" and ea is not None:
+                clip(ea, arg)
+            elif name == "Ea" and ea is not None:
+                clip(ea, arg // 2, (slice(arg % 2, arg % 2 + 1),))
+            elif name == "Cb" and eb is not None:
+                clip(eb, arg)
+            elif name == "Oa" and ea is not None:
+                out_turn(ea, arg)
+            elif name == "Ob" and eb is not None:
+                out_turn(eb, arg)
+            elif name == "Pa" and ea is not None:
+                out_copy(ea, arg)
+            elif name == "Pb" and lt is not None:
+                out_copy(lt, arg)
+            elif name == "Xa" and na is not None:
+                x_turn(na)
+            elif name == "Xb" and nb is not None:
+                x_turn(nb)
+            elif name == "Ya" and na is not None:
+                x_turn_copy(na)
+            elif name == "Yb" and nb is not None:
+                x_turn_copy(nb)
+
+        for tok in HEAD:
+            head_token(tok)
+        for c in range(1, CHUNKS + 2):
+            for tok in TAIL[c] if c in TAIL else STEP:
+                step_token(tok, c)

from contextlib import ExitStack

import concourse.mybir as mybir
from concourse.masks import make_identity

SIZE = 1024
P = 128
CW = [256, 256, 256, 128, 128]
C0 = [0, 256, 512, 768, 896]
CHUNKS = len(CW)
C_LOGISTIC = 1.702
FLOPS = 4 * SIZE * SIZE * SIZE

F32 = mybir.dt.float32
BF16 = mybir.dt.bfloat16
U32 = mybir.dt.uint32
I32 = mybir.dt.int32
U8 = mybir.dt.uint8
FP8 = mybir.dt.float8_e4m3fn
FP8X4 = mybir.dt.float8_e4m3fn_x4
FP4X4 = mybir.dt.float4_e2m1fn_x4
ADD = mybir.AluOpType.add
SUB = mybir.AluOpType.subtract
MUL = mybir.AluOpType.mult
MAX = mybir.AluOpType.max
MIN = mybir.AluOpType.min
ACT = mybir.ActivationFunctionType


def tile_fewbitadclogisticscoreunfoldedstep_d1p_kernel(
    tc, x, p, h_bytes, h_scale, lo, width, g, w_words, w_scales, out
):
    nc = tc.nc
    with ExitStack() as ctx:
        keep = ctx.enter_context(tc.tile_pool(name="keep", bufs=1))
        work = ctx.enter_context(tc.tile_pool(name="work", bufs=2))
        psum = ctx.enter_context(tc.psum_pool(name="psum", bufs=2))
        ctx.enter_context(tc.manual_schedule())

        x_v = x.rearrange("(g p t) b -> g p t b", p=P, t=4)
        lo_v = lo.rearrange("(g p t) b -> g p t b", p=P, t=4)
        wd_v = width.rearrange("(g p t) b -> g p t b", p=P, t=4)
        h_v = h_bytes.rearrange("(g p t) k -> g p t k", p=P, t=4)
        out_v = out.rearrange("(g p t) b -> g p t b", p=P, t=4)

        hs = keep.tile([P, 2, 32], F32)
        p_sb = keep.tile([P, 2, 4], BF16)
        g_sb = keep.tile([P, 2, 4], BF16)
        hb = {}
        for gg in range(2):
            for tp in range(2):
                hb_t = keep.tile([P, 2, SIZE], U8, name=f"hb{gg}{tp}")
                hb[(gg, tp)] = hb_t
        xs, los, wds = {}, {}, {}

        def load_planes(store, view, label, gg, c, n):
            first, total = C0[c], sum(CW[c : c + n])
            t_sb = keep.tile([P, 4, total], BF16, name=f"{label}{gg}_{c}")
            nc.sync.dma_start(out=t_sb[:], in_=view[gg][:, :, first : first + total])
            for i in range(c, c + n):
                store[(i, gg)] = t_sb[:, :, C0[i] - first : C0[i] - first + CW[i]]

        def load_h(gg, tp):
            nc.sync.dma_start(out=hb[(gg, tp)][:], in_=h_v[gg][:, 2 * tp : 2 * tp + 2, :])

        nc.sync.dma_start(out=p_sb[:], in_=p.rearrange("(g p t) -> p g t", p=P, t=4))
        nc.sync.dma_start(out=hs[:], in_=h_scale.rearrange("(g p t) j -> p g (t j)", p=P, t=4))
        load_h(0, 0)
        load_planes(xs, x_v, "x", 0, 0, 1)
        load_planes(xs, x_v, "x", 1, 0, 1)
        load_h(0, 1)
        load_planes(los, lo_v, "lo", 0, 0, 1)
        load_planes(wds, wd_v, "wd", 0, 0, 1)
        nc.sync.dma_start(out=g_sb[:], in_=g.rearrange("(g p t) -> p g t", p=P, t=4))
        load_h(1, 0)
        load_h(1, 1)
        load_planes(los, lo_v, "lo", 1, 0, 1)
        load_planes(wds, wd_v, "wd", 1, 0, 1)
        load_planes(xs, x_v, "x", 0, 1, 1)
        load_planes(xs, x_v, "x", 1, 1, 1)
        for gg in range(2):
            load_planes(los, lo_v, "lo", gg, 1, 1)
            load_planes(wds, wd_v, "wd", gg, 1, 1)
        wt = keep.tile([P, 2, 2 * SIZE], U8, align_bytes=64)
        ws = keep.tile([P, 2, SIZE], U8, align_bytes=64)
        nc.gpsimd.memset(ws[:].rearrange("p g n -> p (g n)").bitcast(U32), 0)
        ws_v = w_scales.bitcast(I32).rearrange("g q n -> q g n")
        for q in range(4):
            nc.sync.dma_start(out=ws[32 * q : 32 * q + 4, :, :].bitcast(I32), in_=ws_v[4 * q : 4 * q + 4])
        for gg in range(2):
            nc.sync.dma_start(out=wt[:, gg, :].bitcast(I32), in_=w_words[gg].bitcast(I32))
        for gg in range(2):
            load_planes(xs, x_v, "x", gg, 2, 3)
        for gg in range(2):
            load_planes(los, lo_v, "lo", gg, 2, 3)
            load_planes(wds, wd_v, "wd", gg, 2, 3)

        ident = keep.tile([P, P], F32)
        make_identity(nc, ident[:])
        warm = keep.tile([P, 1], F32)
        nc.vector.memset(warm[:], 0.0)
        nc.scalar.activation(out=warm[:], in_=warm[:], func=ACT.Tanh)

        ident_bf = keep.tile([P, P], BF16)
        nc.vector.tensor_copy(out=ident_bf[:], in_=ident[:])
        diag = keep.tile([P, 8, P], BF16)
        gc = keep.tile([P, 2, 4], F32)

        hw, hx, hi, hq = {}, {}, {}, {}

        def widen(rt, vec):
            gg, t = divmod(rt, 4)
            hw_t = work.tile([P, SIZE], BF16, bufs=8, align_bytes=64)
            hw[rt] = hw_t
            for j in range(8):
                cols = slice(j * P, (j + 1) * P)
                src = hb[(gg, t // 2)][:, t % 2, cols].bitcast(FP8)
                sc = hs[:, gg, t * 8 + j : t * 8 + j + 1]
                if j in vec:
                    nc.vector.tensor_scalar(out=hw_t[:, cols], in0=src, scalar1=sc, scalar2=None, op0=MUL)
                else:
                    nc.scalar.activation(out=hw_t[:, cols], in_=src, func=ACT.Copy, scale=sc)

        def turn(rt):
            hx_t = psum.tile([P, 2, 2, P], F32, tag="do"[rt % 2], name=f"hx{rt}")
            hx[rt] = hx_t
            words = hw[rt][:].bitcast(F32)
            for k in range(2):
                for u in range(2):
                    nc.tensor.transpose(hx_t[:, k, u, :], words[:, 256 * k + u : 256 * (k + 1) : 2], ident[:])

        def h_copy(rt, vec=True):
            hi_t = work.tile([P, 2, P, 4], BF16, bufs=4, align_bytes=64)
            hi[rt] = hi_t
            move = nc.vector.tensor_copy if vec else nc.scalar.copy
            move(
                out=hi_t[:].rearrange("p k r t -> p (k r t)").bitcast(F32).rearrange("p (k r u) -> p k r u", k=2, u=2),
                in_=hx[rt][:].rearrange("p k u r -> p k r u"),
            )

        def h_quant(rt):
            codes = keep.tile([P, 2, P], U32, name=f"hc{rt}", align_bytes=64)
            scales = keep.tile([P, 2, P], U8, name=f"hsc{rt}", align_bytes=64)
            hq[rt] = (codes, scales)
            nc.vector.quantize_mx(
                out=codes[:].rearrange("p k r -> p (k r)").bitcast(FP8X4),
                scales=scales[:].rearrange("p k r -> p (k r)"),
                in_=hi[rt][:].rearrange("p k r t -> p (k r t)"),
            )

        px, xi, xq = {}, {}, {}

        def px_mm(c, gg):
            px_t = psum.tile([P, 4, CW[c]], BF16, tag="a", name=f"px{c}{gg}")
            px[(c, gg)] = px_t
            for t in range(4):
                nc.tensor.matmul(px_t[:, t, :], lhsT=diag[:, 4 * gg + t, :], rhs=xs[(c, gg)][:, t, :], start=True, stop=True)

        def px_copy(c, gg, vec=False):
            xi_t = work.tile([P, CW[c], 4], BF16, bufs=3, align_bytes=64)
            xi[(c, gg)] = xi_t
            src = px[(c, gg)][:].rearrange("p t b -> p b t")
            if vec:
                nc.vector.tensor_copy(out=xi_t[:], in_=src)
            else:
                nc.scalar.copy(out=xi_t[:], in_=src)

        def px_quant(c, gg):
            codes = work.tile([P, CW[c]], U32, tag=f"xc{gg}", name=f"xc{c}{gg}", bufs=3, align_bytes=64)
            scales = work.tile([P, CW[c]], U8, tag=f"xsc{gg}", name=f"xsc{c}{gg}", bufs=3, align_bytes=64)
            xq[(c, gg)] = (codes, scales)
            nc.vector.quantize_mx(
                out=codes[:].bitcast(FP8X4), scales=scales[:], in_=xi[(c, gg)][:].rearrange("p b t -> p (b t)")
            )

        z, a1, a2, t1, rb, ri, rq = {}, {}, {}, {}, {}, {}, {}

        def banks(c):
            n = 512 // CW[c]
            return [(t, n) for t in range(0, 4, n)]

        def busy(bank, count):
            for i in range(count):
                nc.tensor.matmul_mx(
                    out=bank,
                    lhsT=hq[0][0][:, 0, :].bitcast(FP8X4),
                    lhsT_scale=hq[0][1][:, 0, :],
                    rhs=wt[:, 0, :1024].bitcast(FP4X4),
                    rhs_scale=ws[:, 0, :512],
                    start=True,
                    stop=True,
                )

        def z_mm(c, gg, t0, n):
            z_t = psum.tile([P, n, CW[c]], F32, tag="z", name=f"z{c}{gg}{t0}")
            z[(c, gg, t0)] = z_t
            if c > 1:
                busy(z_t[:].rearrange("p t b -> p (t b)"), KN["bz"])
            for t in range(t0, t0 + n):
                hc, hsc = hq[4 * gg + t]
                for k in range(2):
                    xc, xsc = xq[(c, k)]
                    nc.tensor.matmul_mx(
                        out=z_t[:, t - t0, :],
                        lhsT=hc[:, k, :].bitcast(FP8X4),
                        lhsT_scale=hsc[:, k, :],
                        rhs=xc[:].bitcast(FP8X4),
                        rhs_scale=xsc[:],
                        start=(k == 0),
                        stop=(k == 1),
                    )

        def lo_minus_z(c, gg, t0, n):
            if t0 == 0:
                a1_t = work.tile([P, 4, CW[c]], F32, bufs=4)
                a1[(c, gg)] = a1_t
            ts = slice(t0, t0 + n)
            nc.vector.tensor_tensor(out=a1[(c, gg)][:, ts, :], in0=los[(c, gg)][:, ts, :], in1=z[(c, gg, t0)][:], op=SUB)

        def add_width(c, gg):
            a2_t = work.tile([P, 4, CW[c]], F32, bufs=3)
            a2[(c, gg)] = a2_t
            adder = nc.gpsimd if (c, gg) in KN["a2g"] else nc.vector
            adder.tensor_tensor(out=a2_t[:], in0=a1[(c, gg)][:], in1=wds[(c, gg)], op=ADD)

        def tanh_lo(c, gg):
            t1_t = work.tile([P, 4, CW[c]], F32, bufs=3)
            t1[(c, gg)] = t1_t
            nc.scalar.activation(out=t1_t[:], in_=a1[(c, gg)][:], func=ACT.Tanh, scale=C_LOGISTIC / 2)

        def tanh_up(c, gg):
            nc.scalar.activation(out=a2[(c, gg)][:], in_=a2[(c, gg)][:], func=ACT.Tanh, scale=C_LOGISTIC / 2)

        def tanh_sum(c, gg):
            nc.vector.tensor_tensor(out=t1[(c, gg)][:], in0=t1[(c, gg)][:], in1=a2[(c, gg)][:], op=ADD)

        def times_g(c, gg, planes, vec=False):
            if (c, gg) not in rb:
                rb_t = work.tile([P, 4, CW[c]], BF16, bufs=3)
                rb[(c, gg)] = rb_t
            for t in planes:
                dst, src, col = rb[(c, gg)][:, t, :], t1[(c, gg)][:, t, :], gc[:, gg, t : t + 1]
                if vec:
                    nc.vector.tensor_scalar(out=dst, in0=src, scalar1=col, scalar2=None, op0=MUL)
                else:
                    nc.scalar.activation(out=dst, in_=src, func=ACT.Copy, scale=col)

        def r_inter(c, gg, vec=False):
            ri_t = work.tile([P, 4 * CW[c]], BF16, bufs=3, align_bytes=64)
            ri[(c, gg)] = ri_t
            move = nc.vector.tensor_copy if vec else nc.scalar.copy
            move(
                out=ri_t[:].rearrange("p (c i t) -> p c t i", i=4, t=4),
                in_=rb[(c, gg)][:].rearrange("p t (c i) -> p c t i", i=4),
            )

        def r_quant(c, gg):
            codes = work.tile([P, CW[c]], U32, tag=f"rc{gg}", name=f"rc{c}{gg}", bufs=2, align_bytes=64)
            scales = work.tile([P, CW[c]], U8, tag=f"rsc{gg}", name=f"rsc{c}{gg}", bufs=2, align_bytes=64)
            rq[(c, gg)] = (codes, scales)
            nc.vector.quantize_mx(out=codes[:].bitcast(FP8X4), scales=scales[:], in_=ri[(c, gg)][:])

        d, xtp, xt, q, cl, op = {}, {}, {}, {}, {}, {}

        def where(e):
            c = max(i for i in range(CHUNKS) if C0[i] <= e * P)
            return c, slice(e * P - C0[c], (e + 1) * P - C0[c])

        def d_mm(e):
            c, cols = where(e)
            for kh in range(2):
                d_t = psum.tile([P, 512], F32, tag="d", name=f"d{e}{kh}")
                d[(e, kh)] = d_t
                busy(d_t[:], KN["bd"])
                for k in range(2):
                    rc, rsc = rq[(c, k)]
                    nc.tensor.matmul_mx(
                        out=d_t[:],
                        lhsT=rc[:, cols].bitcast(FP8X4),
                        lhsT_scale=rsc[:, cols],
                        rhs=wt[:, k, 1024 * kh : 1024 * (kh + 1)].bitcast(FP4X4),
                        rhs_scale=ws[:, k, 512 * kh : 512 * (kh + 1)],
                        start=(k == 0),
                        stop=(k == 1),
                    )

        def x_turn(e):
            c, cols = where(e)
            xtp_t = psum.tile([P, 2, 4, P], BF16, tag="a", name=f"xtp{e}")
            xtp[e] = xtp_t
            for kh in range(2):
                for t in range(4):
                    nc.tensor.transpose(xtp_t[:, kh, t, :], xs[(c, kh)][:, t, cols], ident_bf[:])

        def x_turn_copy(e, vec=False):
            xt_t = work.tile([P, 2, 4, P], BF16, bufs=3)
            xt[e] = xt_t
            move = nc.vector.tensor_copy if vec else nc.scalar.copy
            move(out=xt_t[:], in_=xtp[e][:])

        def q_sum(e, kh):
            if kh == 0:
                q_t = work.tile([P, 2, 4, P], F32, bufs=3)
                q[e] = q_t
            nc.vector.tensor_tensor(
                out=q[e][:, kh], in0=d[(e, kh)][:].rearrange("b (s t) -> b t s", t=4), in1=xt[e][:, kh], op=ADD
            )

        def clip(e, i, halves=(slice(0, 2),)):
            if i == 0:
                if e not in cl:
                    cl[e] = {}
            if i not in cl[e]:
                cl_t = work.tile([P, 2, 4, P], F32, tag=f"cl{i}", name=f"cl{e}{i}", bufs=3)
                cl[e][i] = cl_t
            low = 2.0 * i - 2.8
            for s in halves:
                engine = nc.gpsimd if (e, i) in KN["gp"] else nc.vector
                engine.tensor_scalar(
                    out=cl[e][i][:, s], in0=q[e][:, s], scalar1=low, scalar2=low + 1.6, op0=MAX, op1=MIN
                )

        def out_turn(e, kh):
            op_t = psum.tile([P, 4, P], F32, tag="o", name=f"o{e}{kh}")
            op[(e, kh)] = op_t
            busy(op_t[:].rearrange("p t b -> p (t b)"), KN["bo"])
            for t in range(4):
                for i in range(3):
                    nc.tensor.matmul(
                        op_t[:, t, :],
                        lhsT=cl[e][i][:, kh, t, :],
                        rhs=ident[:],
                        is_transpose=True,
                        start=(i == 0),
                        stop=(i == 2),
                    )

        def out_copy(e, kh, vec=False):
            ot_t = work.tile([P, 4, P], F32, bufs=4)
            if vec:
                nc.vector.tensor_scalar(out=ot_t[:], in0=op[(e, kh)][:], scalar1=1.25, scalar2=None, op0=MUL)
            else:
                nc.scalar.activation(out=ot_t[:], in_=op[(e, kh)][:], func=ACT.Copy, scale=1.25)
            nc.sync.dma_start(out=out_v[kh][:, :, e * P : (e + 1) * P], in_=ot_t[:])

        HEAD = "DI WD0 WD2 PX00 WD3 PX01 WD1 TR3 WD4 XC00 TR1 TR0 HC1 TR2 PX10 WD5 HC3 WD7 HQ1 TR5 HQ3 HC5 XC01 PX11 XQ00 TR7 GC XC10 HC2 HQ2 HC0 TR4 HC7 HQ0 XQ01 HQ5 ZZ000 ZZ001 WD6 A1000 HC4 A1001 HQ4 XC11 HQ7 TR6 XQ11 HC6 ZZ010 HQ6 ZZ011 T10 A1010 A20 XQ10 ZZ100 A1011 ZZ101 T11 A1100 A21 A1101 PX20 PX21 T20 T21 ZZ110 ZZ111".split()
        STEP = "SU0 XC0 Pb0 XC1 Qa0 Qa1 GS0 SU1 Xb Db Ca0 GV0 Ca2 GV1 XQ0 A1 GS1 Xa XQ1 Pb1 Ca1 Yb AW0 IL0 Qb0 Oa1 AW1 IL1 TL0 QR0 Qb1 Pa1 QR1 Cb0 Oa0 Cb2 Ya Cb1 PX1 TU0 Z0 PX0 Da Ob0 TU1 A0 Z1 TL1 Pa0 Ob1".split()
        TAIL = {5: "Yb SU0 GV0 Ob0 Cb0 SU1 GS0 IL0 Qa0 GV1 Qa1 Qb1 QR0 Ca0 GS1 Xa Pb0 IL1 QR1 Ca1 Qb0 Pb1 Ya Cb1 Da Ca2 Oa1 Oa0 Pa1 Xb Ob1 Cb2 Pa0 Db".split(), 6: "Qa0 Ea0 Ea2 Qa1 Ea4 Ea1 Ea3 Oa0 Ea5 Pa0 Oa1 Pa1".split()}
        KN = {"wv": {0: [0,1], 1: [0,1,2,3], 2: [0,1,2,3,4,5,6,7], 3: [], 4: [0,1], 5: [], 6: [0,1], 7: [0,1]}, "hcs": [0,1,2,4,5,6,7], "xcv": ["00","01","10"], "gv": {(1, 0): 1, (0, 0): 4, (0, 1): 3, (4, 0): 3, (3, 1): 0, (3, 0): 3, (4, 1): 2, (2, 1): 0, (2, 0): 3, (1, 1): 0}, "ilv": ((0, 1), ), "gp": (), "a2g": (), "bo": 0, "bd": 0, "bz": 0}
        outs = []
        tiles = [[e for e in range(8) if where(e)[0] == c] for c in range(CHUNKS)]
        late = {}

        def head_token(tok):
            name, arg = tok[:2], tok[2:]
            if name == "WD":
                widen(int(arg), KN["wv"][int(arg)])
            elif name == "TR":
                turn(int(arg))
            elif name == "HC":
                h_copy(int(arg), vec=int(arg) not in KN["hcs"])
            elif name == "HQ":
                h_quant(int(arg))
            elif name == "PX":
                px_mm(int(arg[0]), int(arg[1]))
            elif name == "XC":
                px_copy(int(arg[0]), int(arg[1]), vec=arg in KN["xcv"])
            elif name == "XQ":
                px_quant(int(arg[0]), int(arg[1]))
            elif name == "ZZ":
                t0, n = banks(int(arg[0]))[int(arg[2])]
                z_mm(int(arg[0]), int(arg[1]), t0, n)
            elif name == "A1":
                t0, n = banks(int(arg[0]))[int(arg[2])]
                lo_minus_z(int(arg[0]), int(arg[1]), t0, n)
            elif name == "A2":
                add_width(0, int(arg))
            elif name == "T1":
                tanh_lo(0, int(arg))
            elif name == "T2":
                tanh_up(0, int(arg))
            elif name == "GC":
                nc.vector.tensor_scalar(out=gc[:], in0=g_sb[:], scalar1=C_LOGISTIC / 2, scalar2=None, op0=MUL)
            elif name == "DI":
                for i in range(8):
                    nc.vector.tensor_scalar(
                        out=diag[:, i, :], in0=ident[:], scalar1=p_sb[:, i // 4, i % 4 : i % 4 + 1], scalar2=None, op0=MUL
                    )
            else:
                raise ValueError(tok)

        def step_token(tok, c):
            prev, nxt = c - 1, c + 1
            es = tiles[c - 2] if 2 <= c < CHUNKS + 2 else []
            en = tiles[c - 1] if c - 1 < CHUNKS else []
            before = tiles[c - 3] if c >= 3 else []
            has_c, has_p, has_n = c < CHUNKS, prev < CHUNKS, nxt < CHUNKS
            ea, eb = (es[0] if es else None), (es[1] if len(es) == 2 else None)
            na, nb = (en[0] if en else None), (en[1] if len(en) == 2 else None)
            lt = before[1] if len(before) == 2 else None
            name, arg = tok[:2], (int(tok[2]) if len(tok) > 2 else 0)
            if name == "SU" and has_p:
                tanh_sum(prev, arg)
            elif name == "GS" and has_p:
                times_g(prev, arg, range(4 - KN["gv"].get((prev, arg), 2)))
            elif name == "GV" and has_p:
                times_g(prev, arg, range(4 - KN["gv"].get((prev, arg), 2), 4), vec=True)
            elif name == "IL" and has_p:
                r_inter(prev, arg, vec=(prev, arg) in KN["ilv"])
            elif name == "QR" and has_p:
                r_quant(prev, arg)
            elif name == "XC" and has_n:
                px_copy(nxt, arg, vec=str(nxt) + str(arg) in KN["xcv"])
            elif name == "XQ" and has_n:
                px_quant(nxt, arg)
            elif name == "PX" and c + 2 < CHUNKS:
                px_mm(c + 2, arg)
            elif name == "Z0" and has_n:
                for t0, n in banks(nxt):
                    z_mm(nxt, 0, t0, n)
            elif name == "Z1" and has_n:
                for t0, n in banks(nxt):
                    z_mm(nxt, 1, t0, n)
            elif name == "A0" and has_n:
                for t0, n in banks(nxt):
                    lo_minus_z(nxt, 0, t0, n)
            elif name == "A1" and has_c:
                for t0, n in banks(c):
                    lo_minus_z(c, 1, t0, n)
            elif name == "AW" and has_c:
                add_width(c, arg)
            elif name == "TL" and has_c:
                tanh_lo(c, arg)
            elif name == "TU" and has_c:
                tanh_up(c, arg)
            elif name == "Da" and na is not None:
                d_mm(na)
            elif name == "Db" and eb is not None:
                d_mm(eb)
            elif name == "Qa" and ea is not None:
                q_sum(ea, arg)
            elif name == "Qb" and eb is not None:
                q_sum(eb, arg)
            elif name == "Ca" and ea is not None:
                clip(ea, arg)
            elif name == "Ea" and ea is not None:
                clip(ea, arg // 2, (slice(arg % 2, arg % 2 + 1),))
            elif name == "Cb" and eb is not None:
                clip(eb, arg)
            elif name == "Oa" and ea is not None:
                out_turn(ea, arg)
            elif name == "Ob" and eb is not None:
                out_turn(eb, arg)
            elif name == "Pa" and ea is not None:
                out_copy(ea, arg)
            elif name == "Pb" and lt is not None:
                out_copy(lt, arg)
            elif name == "Xa" and na is not None:
                x_turn(na)
            elif name == "Xb" and nb is not None:
                x_turn(nb)
            elif name == "Ya" and na is not None:
                x_turn_copy(na)
            elif name == "Yb" and nb is not None:
                x_turn_copy(nb)

        for tok in HEAD:
            head_token(tok)
        for c in range(1, CHUNKS + 2):
            for tok in TAIL[c] if c in TAIL else STEP:
                step_token(tok, c)
